import numpy as np
import ml_dtypes


def mxq(x, axis, fmt="e4m3"):
    dtype, down = {"e4m3": (ml_dtypes.float8_e4m3fn, 7), "e5m2": (ml_dtypes.float8_e5m2, 14)}[fmt]
    v = np.moveaxis(np.asarray(x, np.float32).astype(ml_dtypes.bfloat16).astype(np.float64), axis, -1)
    blocks = v.reshape(v.shape[:-1] + (-1, 32))
    amax = np.abs(blocks).max(-1, keepdims=True)
    byte = np.maximum(np.where(amax > 0, np.frexp(amax)[1] - 1 + 127, 0) - down, 1)
    scale = np.exp2(byte - 127.0)
    codes = (blocks / scale).astype(np.float32).astype(dtype).astype(np.float64)
    return np.moveaxis((codes * scale).reshape(v.shape), -1, axis)


WIDE = False


def mx_kscale(k):
    if not WIDE:
        return np.ones(k)
    levels = np.array([10, -10, 5, -5, 0])
    if k % 512:
        return np.exp2(np.random.permutation(np.resize(levels, k // 32))).repeat(32)
    a = np.empty((k // 512, 16))
    for p in range(k // 512):
        a[p, :8] = np.random.permutation(np.resize(levels, 8))
        for g in range(8):
            far = levels[np.abs(levels - a[p, g]) >= 10]
            a[p, g + 8] = far[np.random.randint(len(far))]
    return np.exp2(a.ravel()).repeat(32)


def f64(x):
    return np.asarray(x).astype(np.float64)


def striped(idx):
    return np.tile(idx.reshape(-1, 16).T, (8, 1)).astype(np.uint16)


def unstriped(offs):
    return offs[:16].T.reshape(-1).astype(np.int64)


def gelu(v):
    return 0.5 * v * (1.0 + np.tanh(np.sqrt(2.0 / np.pi) * (v + 0.044715 * v**3)))


K, T, D, S, V, H, N = 512, 4096, 2, 1024, 512, 512, 256


def setup_inputs():
    n = np.random.standard_normal
    s = mx_kscale(K)[:, None]
    u = mx_kscale(H)
    return {
        "xT": (n((K, T)) * s).astype(np.float32),
        "w1": (n((K, H)) / np.sqrt(K) / s * u).astype(np.float32),
        "w2": (n((H, N)) / np.sqrt(H) / u[:, None]).astype(np.float32),
        "gate": np.tile(np.random.uniform(0.2, 1.0, (D, 1, V)) / np.sqrt(D), (1, N, 1)).astype(np.float32),
        "offs": striped(np.random.permutation(T)[:S]),
        "pos1": striped(np.random.permutation(S)[:V]),
        "pos2": striped(np.random.permutation(S)[:V]),
    }


def reference(xT, w1, w2, gate, offs, pos1, pos2):
    idx = unstriped(offs)
    xq = mxq(f64(xT)[:, idx], 0, "e4m3")
    h = gelu(mxq(f64(w1), 0, "e4m3").T @ xq)
    y = mxq(f64(w2), 0, "e4m3").T @ mxq(h, 0, "e4m3")
    return sum(f64(gate[d]) * y[:, unstriped(p)] for d, p in enumerate((pos1, pos2)))

@@ -1,0 +1,191 @@
+from contextlib import ExitStack
+
+import concourse.mybir as mybir
+
+K, T, D, S, V, H, N = 512, 4096, 2, 1024, 512, 512, 256
+FLOPS = 2 * S * (K * H + H * N)
+
+F32 = mybir.dt.float32
+BF16 = mybir.dt.bfloat16
+U32 = mybir.dt.uint32
+U16 = mybir.dt.uint16
+U8 = mybir.dt.uint8
+FP8X4 = mybir.dt.float8_e4m3fn_x4
+ACT = mybir.ActivationFunctionType
+MULT, ADD = mybir.AluOpType.mult, mybir.AluOpType.add
+
+P = 128
+PACK = 4
+HALF = 512
+PAIR = 256
+CHUNK = 128
+
+
+def tile_picked_sub_mlp_gelu_sub_e_kernel(tc, xT, w1, w2, gate, offs, pos1, pos2, out):
+    nc = tc.nc
+    with ExitStack() as ctx:
+        lists = ctx.enter_context(tc.tile_pool(name="lists", bufs=1))
+        keep = ctx.enter_context(tc.tile_pool(name="keep", bufs=1))
+        hpsum = ctx.enter_context(tc.psum_pool(name="hpsum", bufs=4))
+        ypsum = ctx.enter_context(tc.psum_pool(name="ypsum", bufs=4))
+
+        offs_t = lists.tile([P, S // 16], U16, name="offs_t")
+        pos_t = [lists.tile([P, V // 16], U16, name=f"pos{dd}_t") for dd in range(D)]
+
+        x_view = xT.rearrange("(p j) t -> p j t", j=PACK)
+        planes = [keep.tile([P, T], F32, name=f"plane{j}") for j in range(PACK)]
+        w1_raw = keep.tile([P, PACK, H], F32, name="w1_raw")
+        w2_raw = [keep.tile([P, PACK, P], F32, name=f"w2_raw{m}") for m in range(2)]
+        gates = [keep.tile([P, D, V], F32, name=f"gates{m}") for m in range(2)]
+
+        nc.sync.dma_start(out=planes[0][:], in_=x_view[:, 0, :])
+        nc.sync.dma_start(offs_t[:], offs)
+        nc.sync.dma_start(out=w1_raw[:], in_=w1.rearrange("(p j) c -> p j c", j=PACK))
+        for j in range(1, PACK):
+            nc.sync.dma_start(out=planes[j][:], in_=x_view[:, j, :])
+        w2_view = w2.rearrange("(p j) c -> p j c", j=PACK)
+        for m in range(2):
+            nc.sync.dma_start(out=w2_raw[m][:], in_=w2_view[:, :, m * P : (m + 1) * P])
+        nc.sync.dma_start(pos_t[0][:], pos1)
+        nc.sync.dma_start(pos_t[1][:], pos2)
+        for m in range(2):
+            nc.sync.dma_start(out=gates[m][:], in_=gate[:, m * P : (m + 1) * P, :].rearrange("d p v -> p d v"))
+
+        warm = keep.tile([P, 1], F32, name="warm")
+        warm_out = keep.tile([P, 1], BF16, name="warm_out")
+        nc.vector.memset(warm[:], 0.0)
+        nc.scalar.activation(warm_out[:], warm[:], ACT.Gelu_apprx_tanh)
+
+        xg = [keep.tile([P, HALF, PACK], BF16, name=f"xg{h}", align_bytes=64) for h in range(2)]
+        x_codes = [keep.tile([P, HALF], U32, name=f"x_codes{h}", align_bytes=64) for h in range(2)]
+        x_scales = [keep.tile([P, HALF], U8, name=f"x_scales{h}", align_bytes=64) for h in range(2)]
+        w1_g = keep.tile([P, H * PACK], BF16, name="w1_g", align_bytes=64)
+        w1_codes = keep.tile([P, H], U32, name="w1_codes", align_bytes=64)
+        w1_scales = keep.tile([P, H], U8, name="w1_scales", align_bytes=64)
+        w2_g = keep.tile([P, N, PACK], BF16, name="w2_g", align_bytes=64)
+        w2_codes = keep.tile([P, N], U32, name="w2_codes", align_bytes=64)
+        w2_scales = keep.tile([P, N], U8, name="w2_scales", align_bytes=64)
+        y = [keep.tile([P, S], F32, name=f"y{m}") for m in range(2)]
+        h_bf = [keep.tile([P, PAIR, PACK], BF16, name=f"h_bf{q}", align_bytes=64) for q in range(4)]
+        h_codes = [keep.tile([P, PAIR], U32, name=f"h_codes{q}", align_bytes=64) for q in range(4)]
+        h_scales = [keep.tile([P, PAIR], U8, name=f"h_scales{q}", align_bytes=64) for q in range(4)]
+
+        def gather(j, h):
+            nc.vector.tensor_copy(xg[h][:, :, j], planes[j][:].indirect(offs_t[:, h * 32 : (h + 1) * 32]))
+
+        def interleave_w2(m):
+            nc.vector.tensor_copy(w2_g[:, m * P : (m + 1) * P, :], w2_raw[m][:].rearrange("p j n -> p n j"))
+
+        def quantize(codes, scales, values):
+            nc.vector.quantize_mx(out=codes.bitcast(FP8X4), scales=scales, in_=values.rearrange("p n j -> p (n j)"))
+
+        def quantize_x(q):
+            h, cols = q // 2, slice((q % 2) * PAIR, (q % 2 + 1) * PAIR)
+            quantize(x_codes[h][:, cols], x_scales[h][:, cols], xg[h][:, cols, :])
+
+        def layer1(c):
+            h, cols = c // 4, slice((c % 4) * CHUNK, (c % 4 + 1) * CHUNK)
+            bank = hpsum.tile([P, PACK, CHUNK], F32, name="bank1")
+            for t in range(PACK):
+                nc.tensor.matmul_mx(
+                    out=bank[:, t, :],
+                    lhsT=w1_codes[:, t * P : (t + 1) * P].bitcast(FP8X4),
+                    lhsT_scale=w1_scales[:, t * P : (t + 1) * P],
+                    rhs=x_codes[h][:, cols].bitcast(FP8X4),
+                    rhs_scale=x_scales[h][:, cols],
+                    start=True,
+                    stop=True,
+                )
+            nc.scalar.activation(
+                h_bf[c // 2][:, (c % 2) * CHUNK : (c % 2 + 1) * CHUNK, :], bank[:].rearrange("p t n -> p n t"), ACT.Gelu_apprx_tanh
+            )
+
+        def quantize_h(first, width):
+            q, cols = first // PAIR, slice(first % PAIR, first % PAIR + width)
+            quantize(h_codes[q][:, cols], h_scales[q][:, cols], h_bf[q][:, cols, :])
+
+        def layer2(first, width):
+            q, cols = first // PAIR, slice(first % PAIR, first % PAIR + width)
+            bank = ypsum.tile([P, 2, PAIR], F32, name="bank2")
+            for m in range(2):
+                nc.tensor.matmul_mx(
+                    out=bank[:, m, :width],
+                    lhsT=w2_codes[:, m * P : (m + 1) * P].bitcast(FP8X4),
+                    lhsT_scale=w2_scales[:, m * P : (m + 1) * P],
+                    rhs=h_codes[q][:, cols].bitcast(FP8X4),
+                    rhs_scale=h_scales[q][:, cols],
+                    start=True,
+                    stop=True,
+                )
+            return bank
+
+        def keep_y(bank, first, width, copy):
+            for m in range(2):
+                copy(y[m][:, first : first + width], bank[:, m, :width])
+
+        nc.scalar.copy(
+            w1_g[:].rearrange("p (t m j) -> p m t j", t=PACK, j=PACK),
+            w1_raw[:].rearrange("p j (m t) -> p m t j", t=PACK),
+        )
+        for j in range(PACK - 1):
+            gather(j, 0)
+            gather(j, 1)
+        nc.vector.quantize_mx(out=w1_codes[:].bitcast(FP8X4), scales=w1_scales[:], in_=w1_g[:])
+        gather(3, 0)
+        interleave_w2(0)
+        quantize_x(0)
+        quantize_x(1)
+        nc.vector.tensor_copy(xg[1][:, 0:1, 3], xg[0][:, 0:1, 3])
+        gather(3, 1)
+        interleave_w2(1)
+        layer1(0)
+        layer1(1)
+        layer1(2)
+        layer1(3)
+        quantize(w2_codes[:], w2_scales[:], w2_g[:])
+        quantize_x(2)
+        layer1(4)
+        layer1(5)
+        quantize_h(0, PAIR)
+        b0 = layer2(0, PAIR)
+        quantize_x(3)
+        layer1(6)
+        layer1(7)
+        quantize_h(PAIR, PAIR)
+        b1 = layer2(PAIR, PAIR)
+        keep_y(b0, 0, PAIR, nc.vector.tensor_copy)
+        quantize_h(2 * PAIR, PAIR)
+        b2 = layer2(2 * PAIR, PAIR)
+        keep_y(b1, PAIR, PAIR, nc.vector.tensor_copy)
+        quantize_h(3 * PAIR, CHUNK)
+        b3 = layer2(3 * PAIR, CHUNK)
+        keep_y(b2, 2 * PAIR, PAIR, nc.vector.tensor_copy)
+        quantize_h(3 * PAIR + CHUNK, CHUNK)
+        b4 = layer2(3 * PAIR + CHUNK, CHUNK)
+        keep_y(b3, 3 * PAIR, CHUNK, nc.vector.tensor_copy)
+        keep_y(b4, 3 * PAIR + CHUNK, CHUNK, nc.scalar.copy)
+
+        terms = [[keep.tile([P, V], F32, name=f"term{m}{dd}") for dd in range(D)] for m in range(2)]
+        results = [keep.tile([P, V], F32, name=f"result{m}") for m in range(2)]
+
+        def neighbour(m, dd, v0, width):
+            nc.vector.tensor_tensor(
+                terms[m][dd][:, v0 : v0 + width],
+                y[m][:].indirect(pos_t[dd][:, v0 // 16 : (v0 + width) // 16]),
+                gates[m][:, dd, v0 : v0 + width],
+                MULT,
+            )
+
+        def total(m, v0, width):
+            cols = slice(v0, v0 + width)
+            nc.vector.tensor_tensor(results[m][:, cols], terms[m][0][:, cols], terms[m][1][:, cols], ADD)
+            nc.sync.dma_start(out=out[m * P : (m + 1) * P, cols], in_=results[m][:, cols])
+
+        neighbour(0, 0, 0, V)
+        neighbour(0, 1, 0, V)
+        neighbour(1, 0, 0, V)
+        total(0, 0, V)
+        neighbour(1, 1, 0, V // 2)
+        neighbour(1, 1, V // 2, V // 2)
+        total(1, 0, V // 2)
+        total(1, V // 2, V // 2)

@@ -26,26 +26,26 @@ def tile_picked_sub_mlp_gelu_sub_e_kernel(tc, xT, w1, w2, gate, offs, pos1, pos2
     with ExitStack() as ctx:
         lists = ctx.enter_context(tc.tile_pool(name="lists", bufs=1))
         keep = ctx.enter_context(tc.tile_pool(name="keep", bufs=1))
-        hpsum = ctx.enter_context(tc.psum_pool(name="hpsum", bufs=4))
-        ypsum = ctx.enter_context(tc.psum_pool(name="ypsum", bufs=4))
+        hpsum = ctx.enter_context(tc.psum_pool(name="hpsum", bufs=3))
+        ypsum = ctx.enter_context(tc.psum_pool(name="ypsum", bufs=1))
 
         offs_t = lists.tile([P, S // 16], U16, name="offs_t")
         pos_t = [lists.tile([P, V // 16], U16, name=f"pos{dd}_t") for dd in range(D)]
 
         x_view = xT.rearrange("(p j) t -> p j t", j=PACK)
         planes = [keep.tile([P, T], F32, name=f"plane{j}") for j in range(PACK)]
-        w1_raw = keep.tile([P, PACK, H], F32, name="w1_raw")
-        w2_raw = [keep.tile([P, PACK, P], F32, name=f"w2_raw{m}") for m in range(2)]
+        w1_raw = [keep.tile([P, PACK, H // 2], F32, name=f"w1_raw{b}") for b in range(2)]
+        w2_raw = keep.tile([P, PACK, N], F32, name="w2_raw")
         gates = [keep.tile([P, D, V], F32, name=f"gates{m}") for m in range(2)]
 
-        nc.sync.dma_start(out=planes[0][:], in_=x_view[:, 0, :])
-        nc.sync.dma_start(offs_t[:], offs)
-        nc.sync.dma_start(out=w1_raw[:], in_=w1.rearrange("(p j) c -> p j c", j=PACK))
-        for j in range(1, PACK):
+        w1_view = w1.rearrange("(p j) c -> p j c", j=PACK)
+        for j in range(PACK):
             nc.sync.dma_start(out=planes[j][:], in_=x_view[:, j, :])
-        w2_view = w2.rearrange("(p j) c -> p j c", j=PACK)
-        for m in range(2):
-            nc.sync.dma_start(out=w2_raw[m][:], in_=w2_view[:, :, m * P : (m + 1) * P])
+            if j == 0:
+                nc.sync.dma_start(offs_t[:], offs)
+        for b in range(2):
+            nc.sync.dma_start(out=w1_raw[b][:], in_=w1_view[:, :, b * H // 2 : (b + 1) * H // 2])
+        nc.sync.dma_start(out=w2_raw[:], in_=w2.rearrange("(p j) c -> p j c", j=PACK))
         nc.sync.dma_start(pos_t[0][:], pos1)
         nc.sync.dma_start(pos_t[1][:], pos2)
         for m in range(2):
@@ -73,11 +73,20 @@ def tile_picked_sub_mlp_gelu_sub_e_kernel(tc, xT, w1, w2, gate, offs, pos1, pos2
         def gather(j, h):
             nc.vector.tensor_copy(xg[h][:, :, j], planes[j][:].indirect(offs_t[:, h * 32 : (h + 1) * 32]))
 
-        def interleave_w2(m):
-            nc.vector.tensor_copy(w2_g[:, m * P : (m + 1) * P, :], w2_raw[m][:].rearrange("p j n -> p n j"))
+        def interleave_w1(b):
+            nc.scalar.copy(
+                w1_g[:].rearrange("p (t m j) -> p m t j", t=PACK, j=PACK)[:, b * 64 : (b + 1) * 64, :, :],
+                w1_raw[b][:].rearrange("p j (m t) -> p m t j", t=PACK),
+            )
 
         def quantize(codes, scales, values):
             nc.vector.quantize_mx(out=codes.bitcast(FP8X4), scales=scales, in_=values.rearrange("p n j -> p (n j)"))
+
+        def quantize_w1(t0, count):
+            cols = slice(t0 * P, (t0 + count) * P)
+            nc.vector.quantize_mx(
+                out=w1_codes[:, cols].bitcast(FP8X4), scales=w1_scales[:, cols], in_=w1_g[:, t0 * P * PACK : (t0 + count) * P * PACK]
+            )
 
         def quantize_x(q):
             h, cols = q // 2, slice((q % 2) * PAIR, (q % 2 + 1) * PAIR)
@@ -104,12 +113,12 @@ def tile_picked_sub_mlp_gelu_sub_e_kernel(tc, xT, w1, w2, gate, offs, pos1, pos2
             q, cols = first // PAIR, slice(first % PAIR, first % PAIR + width)
             quantize(h_codes[q][:, cols], h_scales[q][:, cols], h_bf[q][:, cols, :])
 
-        def layer2(first, width):
+        def layer2(first, width, banks):
             q, cols = first // PAIR, slice(first % PAIR, first % PAIR + width)
-            bank = ypsum.tile([P, 2, PAIR], F32, name="bank2")
             for m in range(2):
+                start, bank = banks[m]
                 nc.tensor.matmul_mx(
-                    out=bank[:, m, :width],
+                    out=bank[:, first - start : first - start + width],
                     lhsT=w2_codes[:, m * P : (m + 1) * P].bitcast(FP8X4),
                     lhsT_scale=w2_scales[:, m * P : (m + 1) * P],
                     rhs=h_codes[q][:, cols].bitcast(FP8X4),
@@ -117,53 +126,47 @@ def tile_picked_sub_mlp_gelu_sub_e_kernel(tc, xT, w1, w2, gate, offs, pos1, pos2
                     start=True,
                     stop=True,
                 )
-            return bank
 
-        def keep_y(bank, first, width, copy):
-            for m in range(2):
-                copy(y[m][:, first : first + width], bank[:, m, :width])
+        y0_a = ypsum.tile([P, 512], F32, name="y0_a")
+        y0_b = ypsum.tile([P, 384], F32, name="y0_b")
+        y0_c = ypsum.tile([P, 128], F32, name="y0_c")
+        y1_a = ypsum.tile([P, 512], F32, name="y1_a")
+        y1_b = ypsum.tile([P, 512], F32, name="y1_b")
 
-        nc.scalar.copy(
-            w1_g[:].rearrange("p (t m j) -> p m t j", t=PACK, j=PACK),
-            w1_raw[:].rearrange("p j (m t) -> p m t j", t=PACK),
-        )
-        for j in range(PACK - 1):
+        for j in range(PACK):
             gather(j, 0)
             gather(j, 1)
-        nc.vector.quantize_mx(out=w1_codes[:].bitcast(FP8X4), scales=w1_scales[:], in_=w1_g[:])
-        gather(3, 0)
-        interleave_w2(0)
+        for b in range(2):
+            interleave_w1(b)
+        nc.scalar.copy(w2_g[:], w2_raw[:].rearrange("p j n -> p n j"))
         quantize_x(0)
+        quantize_w1(0, 2)
+        quantize_w1(2, 2)
         quantize_x(1)
-        nc.vector.tensor_copy(xg[1][:, 0:1, 3], xg[0][:, 0:1, 3])
-        gather(3, 1)
-        interleave_w2(1)
-        layer1(0)
-        layer1(1)
-        layer1(2)
-        layer1(3)
-        quantize(w2_codes[:], w2_scales[:], w2_g[:])
+        for c in range(4):
+            layer1(c)
         quantize_x(2)
+        quantize(w2_codes[:], w2_scales[:], w2_g[:])
+        quantize_h(0, PAIR)
         layer1(4)
         layer1(5)
-        quantize_h(0, PAIR)
-        b0 = layer2(0, PAIR)
+        layer2(0, PAIR, ((0, y0_a), (0, y1_a)))
         quantize_x(3)
         layer1(6)
-        layer1(7)
         quantize_h(PAIR, PAIR)
-        b1 = layer2(PAIR, PAIR)
-        keep_y(b0, 0, PAIR, nc.vector.tensor_copy)
+        layer1(7)
+        layer2(PAIR, PAIR, ((0, y0_a), (0, y1_a)))
         quantize_h(2 * PAIR, PAIR)
-        b2 = layer2(2 * PAIR, PAIR)
-        keep_y(b1, PAIR, PAIR, nc.vector.tensor_copy)
+        nc.vector.tensor_copy(y[0][:, :512], y0_a[:])
+        layer2(2 * PAIR, PAIR, ((512, y0_b), (512, y1_b)))
         quantize_h(3 * PAIR, CHUNK)
-        b3 = layer2(3 * PAIR, CHUNK)
-        keep_y(b2, 2 * PAIR, PAIR, nc.vector.tensor_copy)
+        layer2(3 * PAIR, CHUNK, ((512, y0_b), (512, y1_b)))
         quantize_h(3 * PAIR + CHUNK, CHUNK)
-        b4 = layer2(3 * PAIR + CHUNK, CHUNK)
-        keep_y(b3, 3 * PAIR, CHUNK, nc.vector.tensor_copy)
-        keep_y(b4, 3 * PAIR + CHUNK, CHUNK, nc.scalar.copy)
+        layer2(3 * PAIR + CHUNK, CHUNK, ((896, y0_c), (512, y1_b)))
+        nc.vector.tensor_copy(y[0][:, 512:896], y0_b[:])
+        nc.scalar.copy(y[0][:, 896:], y0_c[:])
+        nc.scalar.copy(y[1][:, :512], y1_a[:])
+        nc.scalar.copy(y[1][:, 512:], y1_b[:])
 
         terms = [[keep.tile([P, V], F32, name=f"term{m}{dd}") for dd in range(D)] for m in range(2)]
         results = [keep.tile([P, V], F32, name=f"result{m}") for m in range(2)]

@@ -26,7 +26,7 @@ def tile_picked_sub_mlp_gelu_sub_e_kernel(tc, xT, w1, w2, gate, offs, pos1, pos2
     with ExitStack() as ctx:
         lists = ctx.enter_context(tc.tile_pool(name="lists", bufs=1))
         keep = ctx.enter_context(tc.tile_pool(name="keep", bufs=1))
-        hpsum = ctx.enter_context(tc.psum_pool(name="hpsum", bufs=3))
+        hpsum = ctx.enter_context(tc.psum_pool(name="hpsum", bufs=4))
         ypsum = ctx.enter_context(tc.psum_pool(name="ypsum", bufs=1))
 
         offs_t = lists.tile([P, S // 16], U16, name="offs_t")
@@ -73,10 +73,10 @@ def tile_picked_sub_mlp_gelu_sub_e_kernel(tc, xT, w1, w2, gate, offs, pos1, pos2
         def gather(j, h):
             nc.vector.tensor_copy(xg[h][:, :, j], planes[j][:].indirect(offs_t[:, h * 32 : (h + 1) * 32]))
 
-        def interleave_w1(b):
-            nc.scalar.copy(
-                w1_g[:].rearrange("p (t m j) -> p m t j", t=PACK, j=PACK)[:, b * 64 : (b + 1) * 64, :, :],
-                w1_raw[b][:].rearrange("p j (m t) -> p m t j", t=PACK),
+        def interleave_w1(b, m0, count, copy):
+            copy(
+                w1_g[:].rearrange("p (t m j) -> p m t j", t=PACK, j=PACK)[:, b * 64 + m0 : b * 64 + m0 + count, :, :],
+                w1_raw[b][:].rearrange("p j (m t) -> p m t j", t=PACK)[:, m0 : m0 + count, :, :],
             )
 
         def quantize(codes, scales, values):
@@ -129,32 +129,36 @@ def tile_picked_sub_mlp_gelu_sub_e_kernel(tc, xT, w1, w2, gate, offs, pos1, pos2
 
         y0_a = ypsum.tile([P, 512], F32, name="y0_a")
         y0_b = ypsum.tile([P, 384], F32, name="y0_b")
-        y0_c = ypsum.tile([P, 128], F32, name="y0_c")
         y1_a = ypsum.tile([P, 512], F32, name="y1_a")
         y1_b = ypsum.tile([P, 512], F32, name="y1_b")
 
-        for j in range(PACK):
+        for j in range(PACK - 1):
             gather(j, 0)
             gather(j, 1)
-        for b in range(2):
-            interleave_w1(b)
-        nc.scalar.copy(w2_g[:], w2_raw[:].rearrange("p j n -> p n j"))
+        gather(3, 0)
+        interleave_w1(0, 0, 64, nc.scalar.copy)
+        interleave_w1(1, 0, 24, nc.scalar.copy)
         quantize_x(0)
+        quantize_x(1)
+        interleave_w1(1, 24, 40, nc.vector.tensor_copy)
         quantize_w1(0, 2)
         quantize_w1(2, 2)
-        quantize_x(1)
+        nc.vector.tensor_copy(xg[1][:, 0:1, 3], w1_g[:, 87 * PACK : 87 * PACK + 1])
+        gather(3, 1)
+        nc.scalar.copy(w2_g[:, :P, :], w2_raw[:, :, :P].rearrange("p j n -> p n j"))
         for c in range(4):
             layer1(c)
         quantize_x(2)
+        quantize_x(3)
+        nc.vector.tensor_copy(w2_g[:, P:, :], w2_raw[:, :, P:].rearrange("p j n -> p n j"))
         quantize(w2_codes[:], w2_scales[:], w2_g[:])
         quantize_h(0, PAIR)
         layer1(4)
         layer1(5)
         layer2(0, PAIR, ((0, y0_a), (0, y1_a)))
-        quantize_x(3)
         layer1(6)
-        quantize_h(PAIR, PAIR)
         layer1(7)
+        quantize_h(PAIR, PAIR)
         layer2(PAIR, PAIR, ((0, y0_a), (0, y1_a)))
         quantize_h(2 * PAIR, PAIR)
         nc.vector.tensor_copy(y[0][:, :512], y0_a[:])
@@ -162,9 +166,10 @@ def tile_picked_sub_mlp_gelu_sub_e_kernel(tc, xT, w1, w2, gate, offs, pos1, pos2
         quantize_h(3 * PAIR, CHUNK)
         layer2(3 * PAIR, CHUNK, ((512, y0_b), (512, y1_b)))
         quantize_h(3 * PAIR + CHUNK, CHUNK)
-        layer2(3 * PAIR + CHUNK, CHUNK, ((896, y0_c), (512, y1_b)))
+        y0_c = hpsum.tile([P, PACK, CHUNK], F32, name="bank1")
+        layer2(3 * PAIR + CHUNK, CHUNK, ((896, y0_c[:, 0, :]), (512, y1_b)))
         nc.vector.tensor_copy(y[0][:, 512:896], y0_b[:])
-        nc.scalar.copy(y[0][:, 896:], y0_c[:])
+        nc.scalar.copy(y[0][:, 896:], y0_c[:, 0, :])
         nc.scalar.copy(y[1][:, :512], y1_a[:])
         nc.scalar.copy(y[1][:, 512:], y1_b[:])
 

from contextlib import ExitStack

import concourse.mybir as mybir

K, T, D, S, V, H, N = 512, 4096, 2, 1024, 512, 512, 256
FLOPS = 2 * S * (K * H + H * N)

F32 = mybir.dt.float32
BF16 = mybir.dt.bfloat16
U32 = mybir.dt.uint32
U16 = mybir.dt.uint16
U8 = mybir.dt.uint8
FP8X4 = mybir.dt.float8_e4m3fn_x4
ACT = mybir.ActivationFunctionType
MULT, ADD = mybir.AluOpType.mult, mybir.AluOpType.add

P = 128
PACK = 4
HALF = 512
PAIR = 256
CHUNK = 128


def tile_picked_sub_mlp_gelu_sub_e_kernel(tc, xT, w1, w2, gate, offs, pos1, pos2, out):
    nc = tc.nc
    with ExitStack() as ctx:
        lists = ctx.enter_context(tc.tile_pool(name="lists", bufs=1))
        keep = ctx.enter_context(tc.tile_pool(name="keep", bufs=1))
        hpsum = ctx.enter_context(tc.psum_pool(name="hpsum", bufs=4))
        ypsum = ctx.enter_context(tc.psum_pool(name="ypsum", bufs=1))

        offs_t = lists.tile([P, S // 16], U16, name="offs_t")
        pos_t = [lists.tile([P, V // 16], U16, name=f"pos{dd}_t") for dd in range(D)]

        x_view = xT.rearrange("(p j) t -> p j t", j=PACK)
        planes = [keep.tile([P, T], F32, name=f"plane{j}") for j in range(PACK)]
        w1_raw = [keep.tile([P, PACK, H // 2], F32, name=f"w1_raw{b}") for b in range(2)]
        w2_raw = keep.tile([P, PACK, N], F32, name="w2_raw")
        gates = [keep.tile([P, D, V], F32, name=f"gates{m}") for m in range(2)]

        w1_view = w1.rearrange("(p j) c -> p j c", j=PACK)
        for j in range(PACK):
            nc.sync.dma_start(out=planes[j][:], in_=x_view[:, j, :])
            if j == 0:
                nc.sync.dma_start(offs_t[:], offs)
        for b in range(2):
            nc.sync.dma_start(out=w1_raw[b][:], in_=w1_view[:, :, b * H // 2 : (b + 1) * H // 2])
        nc.sync.dma_start(out=w2_raw[:], in_=w2.rearrange("(p j) c -> p j c", j=PACK))
        nc.sync.dma_start(pos_t[0][:], pos1)
        nc.sync.dma_start(pos_t[1][:], pos2)
        for m in range(2):
            nc.sync.dma_start(out=gates[m][:], in_=gate[:, m * P : (m + 1) * P, :].rearrange("d p v -> p d v"))

        warm = keep.tile([P, 1], F32, name="warm")
        warm_out = keep.tile([P, 1], BF16, name="warm_out")
        nc.vector.memset(warm[:], 0.0)
        nc.scalar.activation(warm_out[:], warm[:], ACT.Gelu_apprx_tanh)

        xg = [keep.tile([P, HALF, PACK], BF16, name=f"xg{h}", align_bytes=64) for h in range(2)]
        x_codes = [keep.tile([P, HALF], U32, name=f"x_codes{h}", align_bytes=64) for h in range(2)]
        x_scales = [keep.tile([P, HALF], U8, name=f"x_scales{h}", align_bytes=64) for h in range(2)]
        w1_g = keep.tile([P, H * PACK], BF16, name="w1_g", align_bytes=64)
        w1_codes = keep.tile([P, H], U32, name="w1_codes", align_bytes=64)
        w1_scales = keep.tile([P, H], U8, name="w1_scales", align_bytes=64)
        w2_g = keep.tile([P, N, PACK], BF16, name="w2_g", align_bytes=64)
        w2_codes = keep.tile([P, N], U32, name="w2_codes", align_bytes=64)
        w2_scales = keep.tile([P, N], U8, name="w2_scales", align_bytes=64)
        y = [keep.tile([P, S], F32, name=f"y{m}") for m in range(2)]
        h_bf = [keep.tile([P, PAIR, PACK], BF16, name=f"h_bf{q}", align_bytes=64) for q in range(4)]
        h_codes = [keep.tile([P, PAIR], U32, name=f"h_codes{q}", align_bytes=64) for q in range(4)]
        h_scales = [keep.tile([P, PAIR], U8, name=f"h_scales{q}", align_bytes=64) for q in range(4)]

        def gather(j, h):
            nc.vector.tensor_copy(xg[h][:, :, j], planes[j][:].indirect(offs_t[:, h * 32 : (h + 1) * 32]))

        def interleave_w1(b, m0, count, copy):
            copy(
                w1_g[:].rearrange("p (t m j) -> p m t j", t=PACK, j=PACK)[:, b * 64 + m0 : b * 64 + m0 + count, :, :],
                w1_raw[b][:].rearrange("p j (m t) -> p m t j", t=PACK)[:, m0 : m0 + count, :, :],
            )

        def quantize(codes, scales, values):
            nc.vector.quantize_mx(out=codes.bitcast(FP8X4), scales=scales, in_=values.rearrange("p n j -> p (n j)"))

        def quantize_w1(t0, count):
            cols = slice(t0 * P, (t0 + count) * P)
            nc.vector.quantize_mx(
                out=w1_codes[:, cols].bitcast(FP8X4), scales=w1_scales[:, cols], in_=w1_g[:, t0 * P * PACK : (t0 + count) * P * PACK]
            )

        def quantize_x(q):
            h, cols = q // 2, slice((q % 2) * PAIR, (q % 2 + 1) * PAIR)
            quantize(x_codes[h][:, cols], x_scales[h][:, cols], xg[h][:, cols, :])

        def layer1(c):
            h, cols = c // 4, slice((c % 4) * CHUNK, (c % 4 + 1) * CHUNK)
            bank = hpsum.tile([P, PACK, CHUNK], F32, name="bank1")
            for t in range(PACK):
                nc.tensor.matmul_mx(
                    out=bank[:, t, :],
                    lhsT=w1_codes[:, t * P : (t + 1) * P].bitcast(FP8X4),
                    lhsT_scale=w1_scales[:, t * P : (t + 1) * P],
                    rhs=x_codes[h][:, cols].bitcast(FP8X4),
                    rhs_scale=x_scales[h][:, cols],
                    start=True,
                    stop=True,
                )
            nc.scalar.activation(
                h_bf[c // 2][:, (c % 2) * CHUNK : (c % 2 + 1) * CHUNK, :], bank[:].rearrange("p t n -> p n t"), ACT.Gelu_apprx_tanh
            )

        def quantize_h(first, width):
            q, cols = first // PAIR, slice(first % PAIR, first % PAIR + width)
            quantize(h_codes[q][:, cols], h_scales[q][:, cols], h_bf[q][:, cols, :])

        def layer2(first, width, banks):
            q, cols = first // PAIR, slice(first % PAIR, first % PAIR + width)
            for m in range(2):
                start, bank = banks[m]
                nc.tensor.matmul_mx(
                    out=bank[:, first - start : first - start + width],
                    lhsT=w2_codes[:, m * P : (m + 1) * P].bitcast(FP8X4),
                    lhsT_scale=w2_scales[:, m * P : (m + 1) * P],
                    rhs=h_codes[q][:, cols].bitcast(FP8X4),
                    rhs_scale=h_scales[q][:, cols],
                    start=True,
                    stop=True,
                )

        y0_a = ypsum.tile([P, 512], F32, name="y0_a")
        y0_b = ypsum.tile([P, 384], F32, name="y0_b")
        y1_a = ypsum.tile([P, 512], F32, name="y1_a")
        y1_b = ypsum.tile([P, 512], F32, name="y1_b")

        for j in range(PACK - 1):
            gather(j, 0)
            gather(j, 1)
        gather(3, 0)
        interleave_w1(0, 0, 64, nc.scalar.copy)
        interleave_w1(1, 0, 24, nc.scalar.copy)
        quantize_x(0)
        quantize_x(1)
        interleave_w1(1, 24, 40, nc.vector.tensor_copy)
        quantize_w1(0, 2)
        quantize_w1(2, 2)
        nc.vector.tensor_copy(xg[1][:, 0:1, 3], w1_g[:, 87 * PACK : 87 * PACK + 1])
        gather(3, 1)
        nc.scalar.copy(w2_g[:, :P, :], w2_raw[:, :, :P].rearrange("p j n -> p n j"))
        for c in range(4):
            layer1(c)
        quantize_x(2)
        quantize_x(3)
        nc.vector.tensor_copy(w2_g[:, P:, :], w2_raw[:, :, P:].rearrange("p j n -> p n j"))
        quantize(w2_codes[:], w2_scales[:], w2_g[:])
        quantize_h(0, PAIR)
        layer1(4)
        layer1(5)
        layer2(0, PAIR, ((0, y0_a), (0, y1_a)))
        layer1(6)
        layer1(7)
        quantize_h(PAIR, PAIR)
        layer2(PAIR, PAIR, ((0, y0_a), (0, y1_a)))
        quantize_h(2 * PAIR, PAIR)
        nc.vector.tensor_copy(y[0][:, :512], y0_a[:])
        layer2(2 * PAIR, PAIR, ((512, y0_b), (512, y1_b)))
        quantize_h(3 * PAIR, CHUNK)
        layer2(3 * PAIR, CHUNK, ((512, y0_b), (512, y1_b)))
        quantize_h(3 * PAIR + CHUNK, CHUNK)
        y0_c = hpsum.tile([P, PACK, CHUNK], F32, name="bank1")
        layer2(3 * PAIR + CHUNK, CHUNK, ((896, y0_c[:, 0, :]), (512, y1_b)))
        nc.vector.tensor_copy(y[0][:, 512:896], y0_b[:])
        nc.scalar.copy(y[0][:, 896:], y0_c[:, 0, :])
        nc.scalar.copy(y[1][:, :512], y1_a[:])
        nc.scalar.copy(y[1][:, 512:], y1_b[:])

        terms = [[keep.tile([P, V], F32, name=f"term{m}{dd}") for dd in range(D)] for m in range(2)]
        results = [keep.tile([P, V], F32, name=f"result{m}") for m in range(2)]

        def neighbour(m, dd, v0, width):
            nc.vector.tensor_tensor(
                terms[m][dd][:, v0 : v0 + width],
                y[m][:].indirect(pos_t[dd][:, v0 // 16 : (v0 + width) // 16]),
                gates[m][:, dd, v0 : v0 + width],
                MULT,
            )

        def total(m, v0, width):
            cols = slice(v0, v0 + width)
            nc.vector.tensor_tensor(results[m][:, cols], terms[m][0][:, cols], terms[m][1][:, cols], ADD)
            nc.sync.dma_start(out=out[m * P : (m + 1) * P, cols], in_=results[m][:, cols])

        neighbour(0, 0, 0, V)
        neighbour(0, 1, 0, V)
        neighbour(1, 0, 0, V)
        total(0, 0, V)
        neighbour(1, 1, 0, V // 2)
        neighbour(1, 1, V // 2, V // 2)
        total(1, 0, V // 2)
        total(1, V // 2, V // 2)
